import numpy as np
import ml_dtypes


def mxq(x, axis, fmt="e4m3"):
    dtype, down = {"e4m3": (ml_dtypes.float8_e4m3fn, 7), "e5m2": (ml_dtypes.float8_e5m2, 14)}[fmt]
    v = np.moveaxis(np.asarray(x, np.float32).astype(ml_dtypes.bfloat16).astype(np.float64), axis, -1)
    blocks = v.reshape(v.shape[:-1] + (-1, 32))
    amax = np.abs(blocks).max(-1, keepdims=True)
    byte = np.maximum(np.where(amax > 0, np.frexp(amax)[1] - 1 + 127, 0) - down, 1)
    scale = np.exp2(byte - 127.0)
    codes = (blocks / scale).astype(np.float32).astype(dtype).astype(np.float64)
    return np.moveaxis((codes * scale).reshape(v.shape), -1, axis)


WIDE = False


def mx_kscale(k):
    if not WIDE:
        return np.ones(k)
    levels = np.array([10, -10, 5, -5, 0])
    if k % 512:
        return np.exp2(np.random.permutation(np.resize(levels, k // 32))).repeat(32)
    a = np.empty((k // 512, 16))
    for p in range(k // 512):
        a[p, :8] = np.random.permutation(np.resize(levels, 8))
        for g in range(8):
            far = levels[np.abs(levels - a[p, g]) >= 10]
            a[p, g + 8] = far[np.random.randint(len(far))]
    return np.exp2(a.ravel()).repeat(32)


def f64(x):
    return np.asarray(x).astype(np.float64)


def striped8(idx):
    return np.asarray(idx).reshape(8, -1, 16).transpose(0, 2, 1).reshape(128, -1).astype(np.uint16)


def unstriped8(offs):
    return offs.reshape(8, 16, -1).transpose(0, 2, 1).reshape(8, -1).astype(np.int64)


def pick8(x, idx, run):
    r = np.arange(len(x))
    return x[r[:, None], idx[r % (8 * run) // run]]


E2M1 = np.array([0.0, 0.5, 1.0, 1.5, 2.0, 3.0, 4.0, 6.0, -0.0, -0.5, -1.0, -1.5, -2.0, -3.0, -4.0, -6.0])


def pack_weight(w, fmt):
    k, n = w.shape
    w = f64(np.asarray(w, np.float32).astype(ml_dtypes.bfloat16)).reshape(k // 32, 32, n)
    amax = np.abs(w).max(1)
    if fmt == "e4m3":
        byte = np.frexp(amax)[1] - 1 + 127 - 7
    else:
        mant, ex = np.frexp(amax / 6.0)
        byte = np.where(mant > 0.5, ex, ex - 1) + 127
    byte = np.clip(np.where(amax > 0, byte, 1), 1, 254)
    scaled = (w * np.exp2(127.0 - byte)[:, None, :]).reshape(k, n).astype(np.float32)
    by_word = np.ascontiguousarray(scaled.reshape(k // 512, 128, 4, n).transpose(0, 1, 3, 2))
    if fmt == "e4m3":
        words = by_word.astype(ml_dtypes.float8_e4m3fn).view(np.uint8)
    else:
        c = by_word.astype(ml_dtypes.float4_e2m1fn).view(np.uint8) & 0xF
        words = (c[..., 0::2] | (c[..., 1::2] << 4)).reshape(k // 512, 128, 2 * n)
    return np.ascontiguousarray(words), np.ascontiguousarray(byte.astype(np.uint8).reshape(k // 512, 16, n))


def unpack_weight(words, scales, fmt):
    g, _, n = scales.shape
    words = np.ascontiguousarray(words).reshape(g, 128, n, -1)
    if fmt == "e4m3":
        vals = words.view(ml_dtypes.float8_e4m3fn).astype(np.float64)
    else:
        nib = np.empty((g, 128, n, 4), np.uint8)
        nib[..., 0::2] = words & 0xF
        nib[..., 1::2] = words >> 4
        vals = E2M1[nib]
    vals = vals * np.repeat(np.exp2(scales.astype(np.float64) - 127.0), 8, axis=1)[..., None]
    return vals.transpose(0, 1, 3, 2).reshape(g * 512, n)


D, V, Q, I = 512, 2048, 128, 512


def setup_inputs():
    n = np.random.standard_normal
    idx = np.stack([np.random.permutation(V)[:I] for _ in range(8)])
    fd = mx_kscale(D)
    vocp = pack_weight(n((D, V)) / fd[:, None], "e2m1")
    return {
        "hid": (n((D, Q)) * 1.0 / np.sqrt(D) * fd[:, None]).astype(np.float32),
        "voc_words": vocp[0],
        "voc_scales": vocp[1],
        "th": (np.random.uniform(0.0003, 0.001, (Q, 1))).astype(np.float32),
        "sw": (np.random.uniform(0.5, 2.0, (1, I))).astype(np.float32),
        "dhid": (n((D, Q)) * 1.0 / np.sqrt(D) * fd[:, None]).astype(np.float32),
        "base": (0.5 * n((Q, V))).astype(np.float32),
        "offs": striped8(idx),
    }


def reference(hid, voc_words, voc_scales, th, sw, dhid, base, offs):
    idx = unstriped8(offs)
    vocu = unpack_weight(voc_words, voc_scales, "e2m1")
    hidq = mxq(f64(hid), 0, "e4m3")
    a = hidq.T @ vocu
    dhidq = mxq(f64(dhid), 0, "e4m3")
    ta = dhidq.T @ vocu
    m1 = np.max(a, axis=1, keepdims=True)
    p = np.exp(a - m1)
    z = np.sum(p, axis=1, keepdims=True)
    px = np.exp(pick8(a, idx, 16) - m1)
    dpx = f64(sw) / (px + z * f64(th)) - f64(sw) * px / np.square(px + z * f64(th))
    dz = np.sum(f64(sw) * px / np.square(px + z * f64(th)) * (-1.0), axis=1, keepdims=True) * f64(th)
    xp = ta * p
    xz = np.sum(xp, axis=1, keepdims=True)
    xpx = pick8(ta, idx, 16) * px
    xdpx = (xpx + xz * f64(th)) * f64(sw) / np.square(px + z * f64(th)) * (-1.0) - (xpx * f64(sw) - (xpx + xz * f64(th)) * (px + z * f64(th)) * 2.0 * f64(sw) * px / np.square(px + z * f64(th))) / np.square(px + z * f64(th))
    xdz = np.sum((xpx * f64(sw) - (xpx + xz * f64(th)) * (px + z * f64(th)) * 2.0 * f64(sw) * px / np.square(px + z * f64(th))) / np.square(px + z * f64(th)) * (-1.0), axis=1, keepdims=True) * f64(th)
    xe1 = xdpx * px + xpx * dpx
    xs1 = np.zeros((Q, V))
    xs1[np.arange(Q)[:, None], idx[np.arange(Q) % 128 // 16]] = xe1
    xda = xdz * p + xp * dz + xs1
    y = xda * 2.0 + f64(base)
    return y

@@ -1,0 +1,231 @@
+from contextlib import ExitStack
+
+import concourse.mybir as mybir
+from concourse.masks import make_identity
+
+D, V, Q, I = 512, 2048, 128, 512
+FLOPS = 2 * 2 * D * Q * V
+
+F32 = mybir.dt.float32
+BF16 = mybir.dt.bfloat16
+I32 = mybir.dt.int32
+U32 = mybir.dt.uint32
+U16 = mybir.dt.uint16
+U8 = mybir.dt.uint8
+FP8X4 = mybir.dt.float8_e4m3fn_x4
+FP4X4 = mybir.dt.float4_e2m1fn_x4
+ALU = mybir.AluOpType
+ACT = mybir.ActivationFunctionType
+AX = mybir.AxisListType
+
+P = 128
+PACK = 4
+BANK = 512
+NB = V // BANK
+TA_ON_SCALAR = 2
+
+
+def tile_attend_hvpresence_heads_kernel(tc, hid, voc_words, voc_scales, th, sw, dhid, base, offs, out):
+    nc = tc.nc
+    with ExitStack() as ctx:
+        keep = ctx.enter_context(tc.tile_pool(name="keep", bufs=1))
+        psum = ctx.enter_context(tc.psum_pool(name="psum", bufs=1))
+
+        def col(name, n=1):
+            return keep.tile([P, n], F32, name=name)
+
+        voc_sc = keep.tile([P, V], U8, name="voc_sc", align_bytes=64)
+        nc.gpsimd.memset(voc_sc[:].bitcast(I32), 0)
+        warm_in = col("warm_in")
+        warm_out = col("warm_out")
+        nc.vector.memset(warm_in[:], 0.0)
+        nc.scalar.activation(warm_out[:], warm_in[:], ACT.Exp)
+
+        xs = keep.tile([P, V], F32, name="xs")
+        nc.vector.memset(xs[:], 0.0)
+        ident = keep.tile([P, P], F32, name="ident")
+        make_identity(nc, ident[:])
+
+        hid_raw = keep.tile([P, PACK, Q], F32, name="hid_raw")
+        nc.sync.dma_start(out=hid_raw[:], in_=hid.rearrange("(p t) q -> p t q", t=PACK))
+        for quad in range(4):
+            nc.sync.dma_start(
+                out=voc_sc[32 * quad : 32 * quad + 4, :].bitcast(I32),
+                in_=voc_scales[0, 4 * quad : 4 * quad + 4, :].bitcast(I32),
+            )
+        voc_w = [keep.tile([P, V], U8, name="voc_w%d" % half, align_bytes=64) for half in range(2)]
+
+        def load_words(half):
+            nc.sync.dma_start(out=voc_w[half][:].bitcast(I32), in_=voc_words[0, :, half * V : (half + 1) * V].bitcast(I32))
+
+        load_words(0)
+        dhid_raw = keep.tile([P, PACK, Q], F32, name="dhid_raw")
+        nc.sync.dma_start(out=dhid_raw[:], in_=dhid.rearrange("(p t) q -> p t q", t=PACK))
+        load_words(1)
+        offsets = keep.tile([P, I // 16], U16, name="offsets")
+        nc.sync.dma_start(offsets[:], offs)
+        th_c = col("th_c")
+        nc.sync.dma_start(out=th_c[:], in_=th)
+        sw_b = keep.tile([P, I], F32, name="sw_b")
+        nc.sync.dma_start(out=sw_b[:], in_=sw[0].partition_broadcast(P))
+        base_sb = []
+        for half in range(2):
+            b = keep.tile([P, V // 2], F32, name="base%d" % half)
+            nc.sync.dma_start(out=b[:], in_=base[:, half * (V // 2) : (half + 1) * (V // 2)])
+            base_sb.append(b)
+
+        def quantise(name, raw, copy):
+            grouped = keep.tile([P, Q, PACK], BF16, name=name + "_g", align_bytes=64)
+            copy(grouped[:], raw[:].rearrange("p t q -> p q t"))
+            codes = keep.tile([P, Q], U32, name=name + "_codes", align_bytes=64)
+            scales = keep.tile([P, Q], U8, name=name + "_scales", align_bytes=64)
+            nc.vector.quantize_mx(out=codes[:].bitcast(FP8X4), scales=scales[:], in_=grouped[:].rearrange("p q t -> p (q t)"))
+            return codes, scales
+
+        hq = quantise("hid", hid_raw, nc.vector.tensor_copy)
+        dq = quantise("dhid", dhid_raw, nc.scalar.copy)
+
+        def scores(name, operand):
+            banks = []
+            for j in range(NB):
+                bank = psum.tile([P, BANK], F32, name="%s_ps%d" % (name, j), tag="%s_ps%d" % (name, j))
+                words = voc_w[j // 2][:, (j % 2) * 2 * BANK : (j % 2 + 1) * 2 * BANK]
+                nc.tensor.matmul_mx(
+                    out=bank[:],
+                    lhsT=operand[0][:].bitcast(FP8X4),
+                    lhsT_scale=operand[1][:],
+                    rhs=words.bitcast(FP4X4),
+                    rhs_scale=voc_sc[:, j * BANK : (j + 1) * BANK],
+                    start=True,
+                    stop=True,
+                )
+                banks.append(bank)
+            return banks
+
+        a_ps = scores("a", hq)
+        ta_ps = scores("ta", dq)
+
+        def cols(j):
+            return slice(j * BANK, (j + 1) * BANK)
+
+        a_sb = keep.tile([P, V], F32, name="a_sb")
+        ta_sb = keep.tile([P, V], F32, name="ta_sb")
+        p_sb = keep.tile([P, V], F32, name="p_sb")
+        xp_sb = keep.tile([P, V], F32, name="xp_sb")
+        m_b = col("m_b", NB)
+        z_b = col("z_b", NB)
+        xz_b = col("xz_b", NB)
+        for j in range(NB):
+            nc.vector.tensor_scalar(a_sb[:, cols(j)], a_ps[j][:], 1.0, None, ALU.mult, ALU.max, accum_out=m_b[:, j : j + 1])
+            neg_m_j = col("neg_m%d" % j)
+            nc.gpsimd.tensor_scalar(neg_m_j[:], m_b[:, j : j + 1], -1.0, 0.0, ALU.mult, ALU.add)
+            nc.scalar.activation(p_sb[:, cols(j)], a_sb[:, cols(j)], ACT.Exp, bias=neg_m_j[:], accum_out=z_b[:, j : j + 1])
+
+        neg_m = col("neg_m")
+        nc.vector.tensor_reduce(neg_m[:], m_b[:], AX.X, ALU.max, negate=True)
+        a_x = keep.tile([P, I], F32, name="a_x")
+        nc.vector.tensor_copy(a_x[:], a_sb[:].indirect(offsets[:]))
+        f_b = col("f_b", NB)
+        nc.scalar.activation(f_b[:], m_b[:], ACT.Exp, bias=neg_m[:])
+        px = keep.tile([P, I], F32, name="px")
+        nc.scalar.activation(px[:], a_x[:], ACT.Exp, bias=neg_m[:])
+        for j in range(TA_ON_SCALAR):
+            nc.scalar.copy(ta_sb[:, cols(j)], ta_ps[j][:])
+
+        fz_tmp = col("fz_tmp", NB)
+        z = col("z")
+        nc.vector.scalar_tensor_tensor(fz_tmp[:], f_b[:], 1.0, z_b[:], ALU.mult, ALU.mult, accum_out=z[:])
+        rz = col("rz")
+        nc.vector.reciprocal(rz[:], z[:])
+        neg_fz = col("neg_fz", NB)
+        nc.vector.tensor_scalar(neg_fz[:], f_b[:], rz[:], -1.0, ALU.mult, ALU.mult)
+        c = col("c")
+        nc.gpsimd.tensor_scalar(c[:], z[:], th_c[:], 1.0, ALU.mult, ALU.mult)
+        c2 = col("c2")
+        nc.gpsimd.tensor_scalar(c2[:], z[:], th_c[:], 2.0, ALU.mult, ALU.mult)
+        cc2 = col("cc2")
+        nc.gpsimd.tensor_scalar(cc2[:], c[:], c2[:], 1.0, ALU.mult, ALU.mult)
+
+        d_sq = keep.tile([P, I], F32, name="d_sq")
+        nc.scalar.activation(d_sq[:], px[:], ACT.Square, bias=c[:])
+        r_abs = keep.tile([P, I], F32, name="r_abs")
+        nc.scalar.activation(r_abs[:], d_sq[:], ACT.Abs_reciprocal_sqrt)
+        r_sq = keep.tile([P, I], F32, name="r_sq")
+        nc.scalar.activation(r_sq[:], r_abs[:], ACT.Square)
+
+        spx = keep.tile([P, I], F32, name="spx")
+        nc.gpsimd.tensor_tensor(spx[:], px[:], sw_b[:], ALU.mult)
+        cd2 = keep.tile([P, I], F32, name="cd2")
+        nc.gpsimd.tensor_scalar(cd2[:], px[:], c2[:], cc2[:], ALU.mult, ALU.add)
+
+        for j in range(TA_ON_SCALAR, NB):
+            nc.vector.tensor_copy(ta_sb[:, cols(j)], ta_ps[j][:])
+        t_x = keep.tile([P, I], F32, name="t_x")
+        nc.vector.tensor_copy(t_x[:], ta_sb[:].indirect(offsets[:]))
+        for j in range(NB):
+            nc.vector.scalar_tensor_tensor(
+                xp_sb[:, cols(j)], ta_ps[j][:], neg_fz[:, j : j + 1], p_sb[:, cols(j)], ALU.mult, ALU.mult,
+                accum_out=xz_b[:, j : j + 1],
+            )
+        neg_k = col("neg_k")
+        nc.vector.tensor_reduce(neg_k[:], xz_b[:], AX.X, ALU.add)
+
+        g2 = keep.tile([P, I], F32, name="g2")
+        s1 = col("s1")
+        nc.vector.scalar_tensor_tensor(g2[:], spx[:], c2[:], r_sq[:], ALU.mult, ALU.mult, accum_out=s1[:])
+        w2 = keep.tile([P, I], F32, name="w2")
+        nc.vector.tensor_tensor(w2[:], cd2[:], r_sq[:], ALU.mult)
+        h = keep.tile([P, I], F32, name="h", tag="h_y1")
+        nc.vector.scalar_tensor_tensor(h[:], t_x[:], neg_k[:], g2[:], ALU.add, ALU.mult)
+        xe2 = keep.tile([P, I], F32, name="xe2")
+        s2 = col("s2")
+        nc.vector.scalar_tensor_tensor(xe2[:], w2[:], 1.0, h[:], ALU.subtract, ALU.mult, accum_out=s2[:])
+        nc.vector.tensor_copy(xs[:].indirect(offsets[:]), xe2[:])
+
+        def base_cols(j):
+            return base_sb[j // 2][:, (j % 2) * BANK : (j % 2 + 1) * BANK]
+
+        on_tensor = (3, 2)
+        on_gpsimd = (0, 1)
+        bxp = keep.tile([P, V], F32, name="bxp")
+        for j in on_tensor + on_gpsimd:
+            nc.scalar.activation(bxp[:, cols(j)], xp_sb[:, cols(j)], ACT.Identity, scale=s1[:])
+        s_row = col("s_row")
+        nc.scalar.activation(s_row[:], neg_k[:], ACT.Identity, scale=s1[:], bias=s2[:])
+        a_b = col("a_b", NB)
+        nc.scalar.activation(a_b[:], neg_fz[:], ACT.Identity, scale=s_row[:])
+
+        def blocks(ap, b):
+            return ap[:, b * P : (b + 1) * P]
+
+        turned = {}
+        for j in on_tensor:
+            turned[j] = psum.tile([P, BANK], F32, name="turned%d" % j, tag="a_ps%d" % j)
+            for b in range(BANK // P):
+                for n, term in enumerate((base_cols(j), bxp[:, cols(j)])):
+                    nc.tensor.matmul(
+                        blocks(turned[j], b), blocks(term, b), ident[:], start=(n == 0), stop=(n == 1), is_transpose=True
+                    )
+        y1_ps = {}
+        ap = keep.tile([P, len(on_gpsimd) * BANK], F32, name="ap")
+        for j, jg in zip(on_tensor, on_gpsimd):
+            turned_sb = keep.tile([P, BANK], F32, name="turned_sb%d" % j)
+            nc.scalar.copy(turned_sb[:], turned[j][:])
+            nc.scalar.activation(ap[:, cols(jg)], p_sb[:, cols(jg)], ACT.Identity, scale=a_b[:, jg : jg + 1])
+            y1_ps[j] = psum.tile([P, BANK], F32, name="y1_ps%d" % j, tag="a_ps%d" % jg)
+            for b in range(BANK // P):
+                nc.tensor.transpose(blocks(y1_ps[j], b), blocks(turned_sb, b), ident[:])
+
+        y1 = keep.tile([P, len(on_gpsimd) * BANK], F32, name="y1", tag="h_y1")
+        y2 = keep.tile([P, V], F32, name="y2")
+        for j in on_gpsimd:
+            nc.gpsimd.tensor_tensor(y1[:, cols(j)], bxp[:, cols(j)], base_cols(j), ALU.add)
+        for j in on_gpsimd:
+            nc.gpsimd.tensor_tensor(y2[:, cols(j)], y1[:, cols(j)], ap[:, cols(j)], ALU.add)
+
+        res = keep.tile([P, V], F32, name="res")
+        for j in on_tensor:
+            nc.vector.scalar_tensor_tensor(y2[:, cols(j)], p_sb[:, cols(j)], a_b[:, j : j + 1], y1_ps[j][:], ALU.mult, ALU.add)
+        for j in on_tensor + on_gpsimd:
+            nc.vector.tensor_tensor(res[:, cols(j)], y2[:, cols(j)], xs[:, cols(j)], ALU.add)
+            nc.sync.dma_start(out=out[:, cols(j)], in_=res[:, cols(j)])

@@ -22,7 +22,8 @@ P = 128
 PACK = 4
 BANK = 512
 NB = V // BANK
-TA_ON_SCALAR = 2
+TA_ON_SCALAR = 3
+ON_TENSOR = 3
 
 
 def tile_attend_hvpresence_heads_kernel(tc, hid, voc_words, voc_scales, th, sw, dhid, base, offs, out):
@@ -108,43 +109,48 @@ def tile_attend_hvpresence_heads_kernel(tc, hid, voc_words, voc_scales, th, sw, 
         def cols(j):
             return slice(j * BANK, (j + 1) * BANK)
 
+        last = NB - 1
         a_sb = keep.tile([P, V], F32, name="a_sb")
-        ta_sb = keep.tile([P, V], F32, name="ta_sb")
         p_sb = keep.tile([P, V], F32, name="p_sb")
         xp_sb = keep.tile([P, V], F32, name="xp_sb")
-        m_b = col("m_b", NB)
+        m_b = keep.tile([P, NB], F32, name="m_b", tag="m_then_ta")
         z_b = col("z_b", NB)
         xz_b = col("xz_b", NB)
+        f_b = col("f_b", NB)
+        nc.vector.memset(f_b[:, last:NB], 1.0)
+        minus_one = col("minus_one")
+        nc.vector.memset(minus_one[:], -1.0)
+        neg_m = col("neg_m")
         for j in range(NB):
             nc.vector.tensor_scalar(a_sb[:, cols(j)], a_ps[j][:], 1.0, None, ALU.mult, ALU.max, accum_out=m_b[:, j : j + 1])
-            neg_m_j = col("neg_m%d" % j)
-            nc.gpsimd.tensor_scalar(neg_m_j[:], m_b[:, j : j + 1], -1.0, 0.0, ALU.mult, ALU.add)
-            nc.scalar.activation(p_sb[:, cols(j)], a_sb[:, cols(j)], ACT.Exp, bias=neg_m_j[:], accum_out=z_b[:, j : j + 1])
+            if j < last:
+                shift = col("neg_m%d" % j)
+                nc.gpsimd.tensor_scalar(shift[:], m_b[:, j : j + 1], -1.0, 0.0, ALU.mult, ALU.add)
+            else:
+                shift = neg_m
+                nc.vector.tensor_reduce(neg_m[:], m_b[:], AX.X, ALU.max, negate=True)
+            nc.scalar.activation(p_sb[:, cols(j)], a_sb[:, cols(j)], ACT.Exp, bias=shift[:], accum_out=z_b[:, j : j + 1])
 
-        neg_m = col("neg_m")
-        nc.vector.tensor_reduce(neg_m[:], m_b[:], AX.X, ALU.max, negate=True)
         a_x = keep.tile([P, I], F32, name="a_x")
         nc.vector.tensor_copy(a_x[:], a_sb[:].indirect(offsets[:]))
-        f_b = col("f_b", NB)
-        nc.scalar.activation(f_b[:], m_b[:], ACT.Exp, bias=neg_m[:])
+        nc.scalar.activation(f_b[:, :last], m_b[:, :last], ACT.Exp, bias=neg_m[:])
         px = keep.tile([P, I], F32, name="px")
         nc.scalar.activation(px[:], a_x[:], ACT.Exp, bias=neg_m[:])
+        ta_sb = keep.tile([P, V], F32, name="ta_sb", tag="m_then_ta")
         for j in range(TA_ON_SCALAR):
             nc.scalar.copy(ta_sb[:, cols(j)], ta_ps[j][:])
 
         fz_tmp = col("fz_tmp", NB)
         z = col("z")
         nc.vector.scalar_tensor_tensor(fz_tmp[:], f_b[:], 1.0, z_b[:], ALU.mult, ALU.mult, accum_out=z[:])
+        c = col("c")
+        nc.vector.tensor_scalar(c[:], z[:], th_c[:], None, ALU.mult)
         rz = col("rz")
         nc.vector.reciprocal(rz[:], z[:])
+        c2 = col("c2")
+        nc.vector.tensor_scalar(c2[:], z[:], th_c[:], 2.0, ALU.mult, ALU.mult)
         neg_fz = col("neg_fz", NB)
         nc.vector.tensor_scalar(neg_fz[:], f_b[:], rz[:], -1.0, ALU.mult, ALU.mult)
-        c = col("c")
-        nc.gpsimd.tensor_scalar(c[:], z[:], th_c[:], 1.0, ALU.mult, ALU.mult)
-        c2 = col("c2")
-        nc.gpsimd.tensor_scalar(c2[:], z[:], th_c[:], 2.0, ALU.mult, ALU.mult)
-        cc2 = col("cc2")
-        nc.gpsimd.tensor_scalar(cc2[:], c[:], c2[:], 1.0, ALU.mult, ALU.mult)
 
         d_sq = keep.tile([P, I], F32, name="d_sq")
         nc.scalar.activation(d_sq[:], px[:], ACT.Square, bias=c[:])
@@ -153,79 +159,92 @@ def tile_attend_hvpresence_heads_kernel(tc, hid, voc_words, voc_scales, th, sw, 
         r_sq = keep.tile([P, I], F32, name="r_sq")
         nc.scalar.activation(r_sq[:], r_abs[:], ACT.Square)
 
-        spx = keep.tile([P, I], F32, name="spx")
-        nc.gpsimd.tensor_tensor(spx[:], px[:], sw_b[:], ALU.mult)
-        cd2 = keep.tile([P, I], F32, name="cd2")
-        nc.gpsimd.tensor_scalar(cd2[:], px[:], c2[:], cc2[:], ALU.mult, ALU.add)
-
         for j in range(TA_ON_SCALAR, NB):
             nc.vector.tensor_copy(ta_sb[:, cols(j)], ta_ps[j][:])
-        t_x = keep.tile([P, I], F32, name="t_x")
-        nc.vector.tensor_copy(t_x[:], ta_sb[:].indirect(offsets[:]))
         for j in range(NB):
             nc.vector.scalar_tensor_tensor(
                 xp_sb[:, cols(j)], ta_ps[j][:], neg_fz[:, j : j + 1], p_sb[:, cols(j)], ALU.mult, ALU.mult,
                 accum_out=xz_b[:, j : j + 1],
             )
+        t_x = keep.tile([P, I], F32, name="t_x")
+        nc.vector.tensor_copy(t_x[:], ta_sb[:].indirect(offsets[:]))
         neg_k = col("neg_k")
         nc.vector.tensor_reduce(neg_k[:], xz_b[:], AX.X, ALU.add)
+        spx = keep.tile([P, I], F32, name="spx")
+        nc.vector.tensor_tensor(spx[:], px[:], sw_b[:], ALU.mult)
 
+        r = keep.tile([P, I], F32, name="r")
+        nc.vector.scalar_tensor_tensor(r[:], px[:], c[:], r_sq[:], ALU.add, ALU.mult)
         g2 = keep.tile([P, I], F32, name="g2")
         s1 = col("s1")
         nc.vector.scalar_tensor_tensor(g2[:], spx[:], c2[:], r_sq[:], ALU.mult, ALU.mult, accum_out=s1[:])
-        w2 = keep.tile([P, I], F32, name="w2")
-        nc.vector.tensor_tensor(w2[:], cd2[:], r_sq[:], ALU.mult)
-        h = keep.tile([P, I], F32, name="h", tag="h_y1")
+        e = keep.tile([P, I], F32, name="e")
+        nc.scalar.activation(e[:], r[:], ACT.Identity, scale=c2[:], bias=minus_one[:])
+        h = keep.tile([P, I], F32, name="h")
         nc.vector.scalar_tensor_tensor(h[:], t_x[:], neg_k[:], g2[:], ALU.add, ALU.mult)
         xe2 = keep.tile([P, I], F32, name="xe2")
         s2 = col("s2")
-        nc.vector.scalar_tensor_tensor(xe2[:], w2[:], 1.0, h[:], ALU.subtract, ALU.mult, accum_out=s2[:])
+        nc.vector.scalar_tensor_tensor(xe2[:], e[:], 1.0, h[:], ALU.mult, ALU.mult, accum_out=s2[:])
         nc.vector.tensor_copy(xs[:].indirect(offsets[:]), xe2[:])
 
         def base_cols(j):
             return base_sb[j // 2][:, (j % 2) * BANK : (j % 2 + 1) * BANK]
 
-        on_tensor = (3, 2)
-        on_gpsimd = (0, 1)
-        bxp = keep.tile([P, V], F32, name="bxp")
-        for j in on_tensor + on_gpsimd:
+        def block(ap, b):
+            return ap[:, b * P : (b + 1) * P]
+
+        bxp = keep.tile([P, ON_TENSOR * BANK], F32, name="bxp")
+        for j in range(ON_TENSOR):
             nc.scalar.activation(bxp[:, cols(j)], xp_sb[:, cols(j)], ACT.Identity, scale=s1[:])
         s_row = col("s_row")
         nc.scalar.activation(s_row[:], neg_k[:], ACT.Identity, scale=s1[:], bias=s2[:])
         a_b = col("a_b", NB)
         nc.scalar.activation(a_b[:], neg_fz[:], ACT.Identity, scale=s_row[:])
 
-        def blocks(ap, b):
-            return ap[:, b * P : (b + 1) * P]
+        y1 = {}
+        for j in range(ON_TENSOR, NB):
+            y1[j] = keep.tile([P, BANK], F32, name="y1_%d" % j)
+            nc.vector.scalar_tensor_tensor(y1[j][:], xp_sb[:, cols(j)], s1[:], base_cols(j), ALU.mult, ALU.add)
 
         turned = {}
-        for j in on_tensor:
-            turned[j] = psum.tile([P, BANK], F32, name="turned%d" % j, tag="a_ps%d" % j)
+
+        def turn(j):
+            turned[j] = psum.tile([P, BANK], F32, name="turned%d" % j, tag="a_ps%d" % (j % 2))
             for b in range(BANK // P):
                 for n, term in enumerate((base_cols(j), bxp[:, cols(j)])):
                     nc.tensor.matmul(
-                        blocks(turned[j], b), blocks(term, b), ident[:], start=(n == 0), stop=(n == 1), is_transpose=True
+                        block(turned[j], b), block(term, b), ident[:], start=(n == 0), stop=(n == 1), is_transpose=True
                     )
-        y1_ps = {}
-        ap = keep.tile([P, len(on_gpsimd) * BANK], F32, name="ap")
-        for j, jg in zip(on_tensor, on_gpsimd):
+
+        def turn_back(j):
             turned_sb = keep.tile([P, BANK], F32, name="turned_sb%d" % j)
             nc.scalar.copy(turned_sb[:], turned[j][:])
-            nc.scalar.activation(ap[:, cols(jg)], p_sb[:, cols(jg)], ACT.Identity, scale=a_b[:, jg : jg + 1])
-            y1_ps[j] = psum.tile([P, BANK], F32, name="y1_ps%d" % j, tag="a_ps%d" % jg)
+            y1[j] = psum.tile([P, BANK], F32, name="y1_ps%d" % j, tag="ta_ps%d" % j)
             for b in range(BANK // P):
-                nc.tensor.transpose(blocks(y1_ps[j], b), blocks(turned_sb, b), ident[:])
+                nc.tensor.transpose(block(y1[j], b), block(turned_sb, b), ident[:])
 
-        y1 = keep.tile([P, len(on_gpsimd) * BANK], F32, name="y1", tag="h_y1")
+        for step in range(ON_TENSOR + 2):
+            if step >= 2:
+                turn_back(step - 2)
+            if step < ON_TENSOR:
+                turn(step)
+
         y2 = keep.tile([P, V], F32, name="y2")
-        for j in on_gpsimd:
-            nc.gpsimd.tensor_tensor(y1[:, cols(j)], bxp[:, cols(j)], base_cols(j), ALU.add)
-        for j in on_gpsimd:
-            nc.gpsimd.tensor_tensor(y2[:, cols(j)], y1[:, cols(j)], ap[:, cols(j)], ALU.add)
-
         res = keep.tile([P, V], F32, name="res")
-        for j in on_tensor:
-            nc.vector.scalar_tensor_tensor(y2[:, cols(j)], p_sb[:, cols(j)], a_b[:, j : j + 1], y1_ps[j][:], ALU.mult, ALU.add)
-        for j in on_tensor + on_gpsimd:
-            nc.vector.tensor_tensor(res[:, cols(j)], y2[:, cols(j)], xs[:, cols(j)], ALU.add)
-            nc.sync.dma_start(out=out[:, cols(j)], in_=res[:, cols(j)])
+        order = [0, last, 1, 2] if ON_TENSOR < NB else list(range(NB))
+
+        def add_p(j):
+            nc.vector.scalar_tensor_tensor(y2[:, cols(j)], p_sb[:, cols(j)], a_b[:, j : j + 1], y1[j][:], ALU.mult, ALU.add)
+
+        def finish(lo, hi):
+            nc.vector.tensor_tensor(res[:, lo:hi], y2[:, lo:hi], xs[:, lo:hi], ALU.add)
+            nc.sync.dma_start(out=out[:, lo:hi], in_=res[:, lo:hi])
+
+        add_p(order[0])
+        for n, j in enumerate(order):
+            if n + 1 < NB:
+                add_p(order[n + 1])
+                finish(j * BANK, (j + 1) * BANK)
+            else:
+                finish(j * BANK, j * BANK + BANK // 2)
+                finish(j * BANK + BANK // 2, (j + 1) * BANK)

@@ -22,8 +22,10 @@ P = 128
 PACK = 4
 BANK = 512
 NB = V // BANK
-TA_ON_SCALAR = 3
-ON_TENSOR = 3
+TA_ON_SCALAR = 2
+THREE_TERMS = (3,)
+TWO_TERMS = (1, 2)
+ON_VECTOR = (0,)
 
 
 def tile_attend_hvpresence_heads_kernel(tc, hid, voc_words, voc_scales, th, sw, dhid, base, offs, out):
@@ -49,23 +51,23 @@ def tile_attend_hvpresence_heads_kernel(tc, hid, voc_words, voc_scales, th, sw, 
 
         hid_raw = keep.tile([P, PACK, Q], F32, name="hid_raw")
         nc.sync.dma_start(out=hid_raw[:], in_=hid.rearrange("(p t) q -> p t q", t=PACK))
-        for quad in range(4):
-            nc.sync.dma_start(
-                out=voc_sc[32 * quad : 32 * quad + 4, :].bitcast(I32),
-                in_=voc_scales[0, 4 * quad : 4 * quad + 4, :].bitcast(I32),
-            )
         voc_w = [keep.tile([P, V], U8, name="voc_w%d" % half, align_bytes=64) for half in range(2)]
 
         def load_words(half):
             nc.sync.dma_start(out=voc_w[half][:].bitcast(I32), in_=voc_words[0, :, half * V : (half + 1) * V].bitcast(I32))
 
         load_words(0)
+        for quad in range(4):
+            nc.sync.dma_start(
+                out=voc_sc[32 * quad : 32 * quad + 4, :].bitcast(I32),
+                in_=voc_scales[0, 4 * quad : 4 * quad + 4, :].bitcast(I32),
+            )
         dhid_raw = keep.tile([P, PACK, Q], F32, name="dhid_raw")
         nc.sync.dma_start(out=dhid_raw[:], in_=dhid.rearrange("(p t) q -> p t q", t=PACK))
         load_words(1)
         offsets = keep.tile([P, I // 16], U16, name="offsets")
         nc.sync.dma_start(offsets[:], offs)
-        th_c = col("th_c")
+        th_c = keep.tile([P, 1], F32, name="th_c", tag="th_then_spx")
         nc.sync.dma_start(out=th_c[:], in_=th)
         sw_b = keep.tile([P, I], F32, name="sw_b")
         nc.sync.dma_start(out=sw_b[:], in_=sw[0].partition_broadcast(P))
@@ -86,10 +88,10 @@ def tile_attend_hvpresence_heads_kernel(tc, hid, voc_words, voc_scales, th, sw, 
         hq = quantise("hid", hid_raw, nc.vector.tensor_copy)
         dq = quantise("dhid", dhid_raw, nc.scalar.copy)
 
-        def scores(name, operand):
-            banks = []
-            for j in range(NB):
-                bank = psum.tile([P, BANK], F32, name="%s_ps%d" % (name, j), tag="%s_ps%d" % (name, j))
+        def scores(name, operand, tags, which):
+            banks = {}
+            for j in which:
+                bank = psum.tile([P, BANK], F32, name="%s_ps%d" % (name, j), tag=tags[j])
                 words = voc_w[j // 2][:, (j % 2) * 2 * BANK : (j % 2 + 1) * 2 * BANK]
                 nc.tensor.matmul_mx(
                     out=bank[:],
@@ -100,11 +102,11 @@ def tile_attend_hvpresence_heads_kernel(tc, hid, voc_words, voc_scales, th, sw, 
                     start=True,
                     stop=True,
                 )
-                banks.append(bank)
+                banks[j] = bank
             return banks
 
-        a_ps = scores("a", hq)
-        ta_ps = scores("ta", dq)
+        a_ps = scores("a", hq, ("bank0", "bank1", "bank2", "bank3"), range(NB))
+        ta_ps = scores("ta", dq, ("bank4", "bank5", "bank3", "bank4"), range(2))
 
         def cols(j):
             return slice(j * BANK, (j + 1) * BANK)
@@ -113,78 +115,87 @@ def tile_attend_hvpresence_heads_kernel(tc, hid, voc_words, voc_scales, th, sw, 
         a_sb = keep.tile([P, V], F32, name="a_sb")
         p_sb = keep.tile([P, V], F32, name="p_sb")
         xp_sb = keep.tile([P, V], F32, name="xp_sb")
-        m_b = keep.tile([P, NB], F32, name="m_b", tag="m_then_ta")
+        m_b = col("m_b", NB)
         z_b = col("z_b", NB)
         xz_b = col("xz_b", NB)
         f_b = col("f_b", NB)
         nc.vector.memset(f_b[:, last:NB], 1.0)
-        minus_one = col("minus_one")
-        nc.vector.memset(minus_one[:], -1.0)
         neg_m = col("neg_m")
         for j in range(NB):
             nc.vector.tensor_scalar(a_sb[:, cols(j)], a_ps[j][:], 1.0, None, ALU.mult, ALU.max, accum_out=m_b[:, j : j + 1])
             if j < last:
-                shift = col("neg_m%d" % j)
+                shift = keep.tile([P, 1], F32, name="neg_m%d" % j, tag="shift%d" % j)
                 nc.gpsimd.tensor_scalar(shift[:], m_b[:, j : j + 1], -1.0, 0.0, ALU.mult, ALU.add)
             else:
                 shift = neg_m
                 nc.vector.tensor_reduce(neg_m[:], m_b[:], AX.X, ALU.max, negate=True)
             nc.scalar.activation(p_sb[:, cols(j)], a_sb[:, cols(j)], ACT.Exp, bias=shift[:], accum_out=z_b[:, j : j + 1])
 
+        neg_2th = keep.tile([P, 1], F32, name="neg_2th", tag="shift%d" % (last - 1))
+        nc.gpsimd.tensor_scalar(neg_2th[:], th_c[:], -2.0, 1.0, ALU.mult, ALU.mult)
         a_x = keep.tile([P, I], F32, name="a_x")
         nc.vector.tensor_copy(a_x[:], a_sb[:].indirect(offsets[:]))
         nc.scalar.activation(f_b[:, :last], m_b[:, :last], ACT.Exp, bias=neg_m[:])
         px = keep.tile([P, I], F32, name="px")
         nc.scalar.activation(px[:], a_x[:], ACT.Exp, bias=neg_m[:])
-        ta_sb = keep.tile([P, V], F32, name="ta_sb", tag="m_then_ta")
+        preload = col("preload")
+        nc.scalar.activation(preload[:], px[:, 0:1], ACT.Abs_reciprocal_sqrt, bias=f_b[:, last:NB])
+        ta_sb = keep.tile([P, V], F32, name="ta_sb")
         for j in range(TA_ON_SCALAR):
             nc.scalar.copy(ta_sb[:, cols(j)], ta_ps[j][:])
 
-        fz_tmp = col("fz_tmp", NB)
-        z = col("z")
-        nc.vector.scalar_tensor_tensor(fz_tmp[:], f_b[:], 1.0, z_b[:], ALU.mult, ALU.mult, accum_out=z[:])
-        c = col("c")
-        nc.vector.tensor_scalar(c[:], z[:], th_c[:], None, ALU.mult)
-        rz = col("rz")
-        nc.vector.reciprocal(rz[:], z[:])
-        c2 = col("c2")
-        nc.vector.tensor_scalar(c2[:], z[:], th_c[:], 2.0, ALU.mult, ALU.mult)
-        neg_fz = col("neg_fz", NB)
-        nc.vector.tensor_scalar(neg_fz[:], f_b[:], rz[:], -1.0, ALU.mult, ALU.mult)
+        ta_tags = ("bank4", "bank5", "bank3", "bank4")
+        ta_ps[2] = scores("ta", dq, ta_tags, range(2, 3))[2]
+        nc.vector.tensor_copy(ta_sb[:, cols(2)], ta_ps[2][:])
 
-        d_sq = keep.tile([P, I], F32, name="d_sq")
-        nc.scalar.activation(d_sq[:], px[:], ACT.Square, bias=c[:])
+        fz_tmp = col("fz_tmp", NB)
+        neg_z = col("neg_z")
+        nc.vector.scalar_tensor_tensor(fz_tmp[:], f_b[:], -1.0, z_b[:], ALU.mult, ALU.mult, accum_out=neg_z[:])
+        c = col("c")
+        nc.gpsimd.tensor_scalar(c[:], neg_z[:], th_c[:], -1.0, ALU.mult, ALU.mult)
+        slope = col("slope")
+        nc.gpsimd.tensor_scalar(slope[:], neg_z[:], neg_z[:], neg_2th[:], ALU.mult, ALU.mult)
+        spx = keep.tile([P, I], F32, name="spx", tag="th_then_spx")
+        nc.gpsimd.tensor_tensor(spx[:], px[:], sw_b[:], ALU.mult)
+        shift_c = col("shift_c")
+        nc.gpsimd.tensor_scalar(shift_c[:], slope[:], c[:], 1.0, ALU.mult, ALU.mult)
+
+        r_root = keep.tile([P, I], F32, name="r_root", tag="root_then_cd")
+        nc.scalar.activation(r_root[:], px[:], ACT.Abs_reciprocal_sqrt, bias=c[:])
         r_abs = keep.tile([P, I], F32, name="r_abs")
-        nc.scalar.activation(r_abs[:], d_sq[:], ACT.Abs_reciprocal_sqrt)
+        nc.scalar.activation(r_abs[:], r_root[:], ACT.Square)
         r_sq = keep.tile([P, I], F32, name="r_sq")
         nc.scalar.activation(r_sq[:], r_abs[:], ACT.Square)
+        cd = keep.tile([P, I], F32, name="cd", tag="root_then_cd")
+        nc.scalar.activation(cd[:], px[:], ACT.Identity, scale=slope[:], bias=shift_c[:])
 
-        for j in range(TA_ON_SCALAR, NB):
-            nc.vector.tensor_copy(ta_sb[:, cols(j)], ta_ps[j][:])
+        banks = dict(ta_ps)
         for j in range(NB):
+            if j == last:
+                banks[j] = scores("ta", dq, ta_tags, range(last, NB))[last]
+                nc.vector.tensor_copy(ta_sb[:, cols(j)], banks[j][:])
             nc.vector.scalar_tensor_tensor(
-                xp_sb[:, cols(j)], ta_ps[j][:], neg_fz[:, j : j + 1], p_sb[:, cols(j)], ALU.mult, ALU.mult,
+                xp_sb[:, cols(j)], banks[j][:], f_b[:, j : j + 1], p_sb[:, cols(j)], ALU.mult, ALU.mult,
                 accum_out=xz_b[:, j : j + 1],
             )
         t_x = keep.tile([P, I], F32, name="t_x")
         nc.vector.tensor_copy(t_x[:], ta_sb[:].indirect(offsets[:]))
+        neg_rz = col("neg_rz")
+        nc.vector.reciprocal(neg_rz[:], neg_z[:])
+        k_tmp = col("k_tmp", NB)
         neg_k = col("neg_k")
-        nc.vector.tensor_reduce(neg_k[:], xz_b[:], AX.X, ALU.add)
-        spx = keep.tile([P, I], F32, name="spx")
-        nc.vector.tensor_tensor(spx[:], px[:], sw_b[:], ALU.mult)
+        nc.vector.tensor_scalar(k_tmp[:], xz_b[:], neg_rz[:], None, ALU.mult, ALU.add, accum_out=neg_k[:])
 
-        r = keep.tile([P, I], F32, name="r")
-        nc.vector.scalar_tensor_tensor(r[:], px[:], c[:], r_sq[:], ALU.add, ALU.mult)
-        g2 = keep.tile([P, I], F32, name="g2")
-        s1 = col("s1")
-        nc.vector.scalar_tensor_tensor(g2[:], spx[:], c2[:], r_sq[:], ALU.mult, ALU.mult, accum_out=s1[:])
-        e = keep.tile([P, I], F32, name="e")
-        nc.scalar.activation(e[:], r[:], ACT.Identity, scale=c2[:], bias=minus_one[:])
+        g = keep.tile([P, I], F32, name="g")
+        b_row = col("b_row")
+        nc.vector.scalar_tensor_tensor(g[:], spx[:], neg_2th[:], r_sq[:], ALU.mult, ALU.mult, accum_out=b_row[:])
+        w = keep.tile([P, I], F32, name="w")
+        nc.vector.tensor_tensor(w[:], cd[:], r_sq[:], ALU.mult)
         h = keep.tile([P, I], F32, name="h")
-        nc.vector.scalar_tensor_tensor(h[:], t_x[:], neg_k[:], g2[:], ALU.add, ALU.mult)
+        nc.vector.scalar_tensor_tensor(h[:], t_x[:], neg_k[:], g[:], ALU.add, ALU.mult)
         xe2 = keep.tile([P, I], F32, name="xe2")
         s2 = col("s2")
-        nc.vector.scalar_tensor_tensor(xe2[:], e[:], 1.0, h[:], ALU.mult, ALU.mult, accum_out=s2[:])
+        nc.vector.scalar_tensor_tensor(xe2[:], w[:], neg_z[:], h[:], ALU.subtract, ALU.mult, accum_out=s2[:])
         nc.vector.tensor_copy(xs[:].indirect(offsets[:]), xe2[:])
 
         def base_cols(j):
@@ -193,58 +204,58 @@ def tile_attend_hvpresence_heads_kernel(tc, hid, voc_words, voc_scales, th, sw, 
         def block(ap, b):
             return ap[:, b * P : (b + 1) * P]
 
-        bxp = keep.tile([P, ON_TENSOR * BANK], F32, name="bxp")
-        for j in range(ON_TENSOR):
-            nc.scalar.activation(bxp[:, cols(j)], xp_sb[:, cols(j)], ACT.Identity, scale=s1[:])
-        s_row = col("s_row")
-        nc.scalar.activation(s_row[:], neg_k[:], ACT.Identity, scale=s1[:], bias=s2[:])
+        bxp = keep.tile([P, V], F32, name="bxp")
+        for j in TWO_TERMS + THREE_TERMS:
+            nc.scalar.activation(bxp[:, cols(j)], xp_sb[:, cols(j)], ACT.Identity, scale=b_row[:])
+        kb = col("kb")
+        nc.scalar.activation(kb[:], neg_k[:], ACT.Identity, scale=b_row[:])
+        a_row = col("a_row")
+        nc.scalar.activation(a_row[:], neg_rz[:], ACT.Identity, scale=s2[:], bias=kb[:])
+        ap = keep.tile([P, V], F32, name="ap")
+        nc.scalar.activation(ap[:, cols(last)], p_sb[:, cols(last)], ACT.Identity, scale=a_row[:])
         a_b = col("a_b", NB)
-        nc.scalar.activation(a_b[:], neg_fz[:], ACT.Identity, scale=s_row[:])
+        nc.scalar.activation(a_b[:], f_b[:], ACT.Identity, scale=a_row[:])
 
-        y1 = {}
-        for j in range(ON_TENSOR, NB):
-            y1[j] = keep.tile([P, BANK], F32, name="y1_%d" % j)
-            nc.vector.scalar_tensor_tensor(y1[j][:], xp_sb[:, cols(j)], s1[:], base_cols(j), ALU.mult, ALU.add)
+        partial = {}
+        for j in ON_VECTOR:
+            partial[j] = keep.tile([P, BANK], F32, name="partial%d" % j)
+            nc.vector.scalar_tensor_tensor(partial[j][:], xp_sb[:, cols(j)], b_row[:], base_cols(j), ALU.mult, ALU.add)
 
-        turned = {}
-
-        def turn(j):
-            turned[j] = psum.tile([P, BANK], F32, name="turned%d" % j, tag="a_ps%d" % (j % 2))
+        for j in TWO_TERMS + THREE_TERMS:
+            terms = [base_cols(j), bxp[:, cols(j)]] + ([ap[:, cols(j)]] if j in THREE_TERMS else [])
+            turned = psum.tile([P, BANK], F32, name="turned%d" % j, tag="bank%d" % (j - 1))
             for b in range(BANK // P):
-                for n, term in enumerate((base_cols(j), bxp[:, cols(j)])):
+                for n, term in enumerate(terms):
                     nc.tensor.matmul(
-                        block(turned[j], b), block(term, b), ident[:], start=(n == 0), stop=(n == 1), is_transpose=True
+                        block(turned, b), block(term, b), ident[:],
+                        start=(n == 0), stop=(n == len(terms) - 1), is_transpose=True,
                     )
-
-        def turn_back(j):
             turned_sb = keep.tile([P, BANK], F32, name="turned_sb%d" % j)
-            nc.scalar.copy(turned_sb[:], turned[j][:])
-            y1[j] = psum.tile([P, BANK], F32, name="y1_ps%d" % j, tag="ta_ps%d" % j)
+            nc.scalar.copy(turned_sb[:], turned[:])
+            partial[j] = psum.tile([P, BANK], F32, name="partial_ps%d" % j, tag="bank%d" % (j + 4))
             for b in range(BANK // P):
-                nc.tensor.transpose(block(y1[j], b), block(turned_sb, b), ident[:])
+                nc.tensor.transpose(block(partial[j], b), block(turned_sb, b), ident[:])
 
-        for step in range(ON_TENSOR + 2):
-            if step >= 2:
-                turn_back(step - 2)
-            if step < ON_TENSOR:
-                turn(step)
-
-        y2 = keep.tile([P, V], F32, name="y2")
+        dense = keep.tile([P, V], F32, name="dense")
         res = keep.tile([P, V], F32, name="res")
-        order = [0, last, 1, 2] if ON_TENSOR < NB else list(range(NB))
 
         def add_p(j):
-            nc.vector.scalar_tensor_tensor(y2[:, cols(j)], p_sb[:, cols(j)], a_b[:, j : j + 1], y1[j][:], ALU.mult, ALU.add)
+            nc.vector.scalar_tensor_tensor(
+                dense[:, cols(j)], p_sb[:, cols(j)], a_b[:, j : j + 1], partial[j][:], ALU.mult, ALU.add
+            )
 
-        def finish(lo, hi):
-            nc.vector.tensor_tensor(res[:, lo:hi], y2[:, lo:hi], xs[:, lo:hi], ALU.add)
-            nc.sync.dma_start(out=out[:, lo:hi], in_=res[:, lo:hi])
+        def finish(j, lo, hi):
+            src = partial[j][:, lo:hi] if j in THREE_TERMS else dense[:, j * BANK + lo : j * BANK + hi]
+            span = slice(j * BANK + lo, j * BANK + hi)
+            nc.vector.tensor_tensor(res[:, span], src, xs[:, span], ALU.add)
+            nc.sync.dma_start(out=out[:, span], in_=res[:, span])
 
-        add_p(order[0])
+        order = ON_VECTOR + TWO_TERMS + THREE_TERMS
         for n, j in enumerate(order):
+            if j not in THREE_TERMS:
+                add_p(j)
             if n + 1 < NB:
-                add_p(order[n + 1])
-                finish(j * BANK, (j + 1) * BANK)
+                finish(j, 0, BANK)
             else:
-                finish(j * BANK, j * BANK + BANK // 2)
-                finish(j * BANK + BANK // 2, (j + 1) * BANK)
+                finish(j, 0, BANK // 2)
+                finish(j, BANK // 2, BANK)

@@ -161,11 +161,15 @@ def tile_attend_hvpresence_heads_kernel(tc, hid, voc_words, voc_scales, th, sw, 
         nc.gpsimd.tensor_scalar(shift_c[:], slope[:], c[:], 1.0, ALU.mult, ALU.mult)
 
         r_root = keep.tile([P, I], F32, name="r_root", tag="root_then_cd")
-        nc.scalar.activation(r_root[:], px[:], ACT.Abs_reciprocal_sqrt, bias=c[:])
         r_abs = keep.tile([P, I], F32, name="r_abs")
-        nc.scalar.activation(r_abs[:], r_root[:], ACT.Square)
         r_sq = keep.tile([P, I], F32, name="r_sq")
-        nc.scalar.activation(r_sq[:], r_abs[:], ACT.Square)
+        halves = (slice(0, I // 2), slice(I // 2, I))
+        for half in halves:
+            nc.scalar.activation(r_root[:, half], px[:, half], ACT.Abs_reciprocal_sqrt, bias=c[:])
+        for half in halves:
+            nc.scalar.activation(r_abs[:, half], r_root[:, half], ACT.Square)
+        for half in halves:
+            nc.scalar.activation(r_sq[:, half], r_abs[:, half], ACT.Square)
         cd = keep.tile([P, I], F32, name="cd", tag="root_then_cd")
         nc.scalar.activation(cd[:], px[:], ACT.Identity, scale=slope[:], bias=shift_c[:])
 
@@ -230,32 +234,31 @@ def tile_attend_hvpresence_heads_kernel(tc, hid, voc_words, voc_scales, th, sw, 
                         block(turned, b), block(term, b), ident[:],
                         start=(n == 0), stop=(n == len(terms) - 1), is_transpose=True,
                     )
-            turned_sb = keep.tile([P, BANK], F32, name="turned_sb%d" % j)
+            turned_sb = keep.tile([P, BANK], F32, name="turned_sb%d" % j, tag="turned_then_res%d" % j)
             nc.scalar.copy(turned_sb[:], turned[:])
             partial[j] = psum.tile([P, BANK], F32, name="partial_ps%d" % j, tag="bank%d" % (j + 4))
             for b in range(BANK // P):
                 nc.tensor.transpose(block(partial[j], b), block(turned_sb, b), ident[:])
 
         dense = keep.tile([P, V], F32, name="dense")
-        res = keep.tile([P, V], F32, name="res")
 
         def add_p(j):
             nc.vector.scalar_tensor_tensor(
                 dense[:, cols(j)], p_sb[:, cols(j)], a_b[:, j : j + 1], partial[j][:], ALU.mult, ALU.add
             )
 
-        def finish(j, lo, hi):
-            src = partial[j][:, lo:hi] if j in THREE_TERMS else dense[:, j * BANK + lo : j * BANK + hi]
-            span = slice(j * BANK + lo, j * BANK + hi)
-            nc.vector.tensor_tensor(res[:, span], src, xs[:, span], ALU.add)
-            nc.sync.dma_start(out=out[:, span], in_=res[:, span])
+        def finish(j, src, tag, pieces):
+            res = keep.tile([P, BANK], F32, name="res%d" % j, tag=tag)
+            width = BANK // pieces
+            for lo in range(0, BANK, width):
+                span = slice(j * BANK + lo, j * BANK + lo + width)
+                nc.vector.tensor_tensor(res[:, lo : lo + width], src[:, lo : lo + width], xs[:, span], ALU.add)
+                nc.sync.dma_start(out=out[:, span], in_=res[:, lo : lo + width])
 
-        order = ON_VECTOR + TWO_TERMS + THREE_TERMS
-        for n, j in enumerate(order):
-            if j not in THREE_TERMS:
-                add_p(j)
-            if n + 1 < NB:
-                finish(j, 0, BANK)
-            else:
-                finish(j, 0, BANK // 2)
-                finish(j, BANK // 2, BANK)
+        add_p(0)
+        add_p(1)
+        finish(0, dense[:, cols(0)], "turned_then_res1", 1)
+        add_p(2)
+        finish(1, dense[:, cols(1)], "turned_then_res2", 1)
+        finish(3, partial[3], "res3", 1)
+        finish(2, dense[:, cols(2)], "turned_then_res3", 2)

@@ -20,12 +20,12 @@ AX = mybir.AxisListType
 
 P = 128
 PACK = 4
-BANK = 512
-NB = V // BANK
+CHUNK = 512
+CHUNKS = V // CHUNK
+LAST = CHUNKS - 1
+HALF = CHUNK // 2
+TA_BANKS = ("bank4", "bank5", "bank3", "bank4")
 TA_ON_SCALAR = 2
-THREE_TERMS = (3,)
-TWO_TERMS = (1, 2)
-ON_VECTOR = (0,)
 
 
 def tile_attend_hvpresence_heads_kernel(tc, hid, voc_words, voc_scales, th, sw, dhid, base, offs, out):
@@ -34,19 +34,24 @@ def tile_attend_hvpresence_heads_kernel(tc, hid, voc_words, voc_scales, th, sw, 
         keep = ctx.enter_context(tc.tile_pool(name="keep", bufs=1))
         psum = ctx.enter_context(tc.psum_pool(name="psum", bufs=1))
 
-        def col(name, n=1):
-            return keep.tile([P, n], F32, name=name)
+        def wide(name, width, tag=""):
+            return keep.tile([P, width], F32, name=name, tag=tag or name)
+
+        def cols(j):
+            return slice(j * CHUNK, (j + 1) * CHUNK)
+
+        def block(rows, n):
+            return rows[:, n * P : (n + 1) * P]
 
         voc_sc = keep.tile([P, V], U8, name="voc_sc", align_bytes=64)
         nc.gpsimd.memset(voc_sc[:].bitcast(I32), 0)
-        warm_in = col("warm_in")
-        warm_out = col("warm_out")
-        nc.vector.memset(warm_in[:], 0.0)
-        nc.scalar.activation(warm_out[:], warm_in[:], ACT.Exp)
-
-        xs = keep.tile([P, V], F32, name="xs")
-        nc.vector.memset(xs[:], 0.0)
-        ident = keep.tile([P, P], F32, name="ident")
+        zero = wide("zero", 1)
+        f = wide("f", CHUNKS)
+        nc.vector.memset(zero[:], 0.0)
+        nc.scalar.activation(f[:, LAST:CHUNKS], zero[:], ACT.Exp)
+        scattered = wide("scattered", V)
+        nc.vector.memset(scattered[:], 0.0)
+        ident = wide("ident", P)
         make_identity(nc, ident[:])
 
         hid_raw = keep.tile([P, PACK, Q], F32, name="hid_raw")
@@ -57,208 +62,201 @@ def tile_attend_hvpresence_heads_kernel(tc, hid, voc_words, voc_scales, th, sw, 
             nc.sync.dma_start(out=voc_w[half][:].bitcast(I32), in_=voc_words[0, :, half * V : (half + 1) * V].bitcast(I32))
 
         load_words(0)
-        for quad in range(4):
+        for quadrant in range(4):
             nc.sync.dma_start(
-                out=voc_sc[32 * quad : 32 * quad + 4, :].bitcast(I32),
-                in_=voc_scales[0, 4 * quad : 4 * quad + 4, :].bitcast(I32),
+                out=voc_sc[32 * quadrant : 32 * quadrant + 4, :].bitcast(I32),
+                in_=voc_scales[0, 4 * quadrant : 4 * quadrant + 4, :].bitcast(I32),
             )
         dhid_raw = keep.tile([P, PACK, Q], F32, name="dhid_raw")
         nc.sync.dma_start(out=dhid_raw[:], in_=dhid.rearrange("(p t) q -> p t q", t=PACK))
         load_words(1)
         offsets = keep.tile([P, I // 16], U16, name="offsets")
         nc.sync.dma_start(offsets[:], offs)
-        th_c = keep.tile([P, 1], F32, name="th_c", tag="th_then_spx")
-        nc.sync.dma_start(out=th_c[:], in_=th)
-        sw_b = keep.tile([P, I], F32, name="sw_b")
-        nc.sync.dma_start(out=sw_b[:], in_=sw[0].partition_broadcast(P))
-        base_sb = []
+        th_col = wide("th_col", 1, tag="th_then_sw_px")
+        nc.sync.dma_start(out=th_col[:], in_=th)
+        sw_rows = wide("sw_rows", I)
+        nc.sync.dma_start(out=sw_rows[:], in_=sw[0].partition_broadcast(P))
+        base_halves = []
         for half in range(2):
-            b = keep.tile([P, V // 2], F32, name="base%d" % half)
-            nc.sync.dma_start(out=b[:], in_=base[:, half * (V // 2) : (half + 1) * (V // 2)])
-            base_sb.append(b)
+            base_half = wide("base%d" % half, V // 2)
+            nc.sync.dma_start(out=base_half[:], in_=base[:, half * (V // 2) : (half + 1) * (V // 2)])
+            base_halves.append(base_half)
+
+        def base_chunk(j):
+            return base_halves[j // 2][:, cols(j % 2)]
 
         def quantise(name, raw, copy):
-            grouped = keep.tile([P, Q, PACK], BF16, name=name + "_g", align_bytes=64)
+            grouped = keep.tile([P, Q, PACK], BF16, name=name + "_grouped", align_bytes=64)
             copy(grouped[:], raw[:].rearrange("p t q -> p q t"))
             codes = keep.tile([P, Q], U32, name=name + "_codes", align_bytes=64)
             scales = keep.tile([P, Q], U8, name=name + "_scales", align_bytes=64)
             nc.vector.quantize_mx(out=codes[:].bitcast(FP8X4), scales=scales[:], in_=grouped[:].rearrange("p q t -> p (q t)"))
             return codes, scales
 
-        hq = quantise("hid", hid_raw, nc.vector.tensor_copy)
-        dq = quantise("dhid", dhid_raw, nc.scalar.copy)
+        hid_mx = quantise("hid", hid_raw, nc.vector.tensor_copy)
+        dhid_mx = quantise("dhid", dhid_raw, nc.scalar.copy)
 
-        def scores(name, operand, tags, which):
-            banks = {}
-            for j in which:
-                bank = psum.tile([P, BANK], F32, name="%s_ps%d" % (name, j), tag=tags[j])
-                words = voc_w[j // 2][:, (j % 2) * 2 * BANK : (j % 2 + 1) * 2 * BANK]
-                nc.tensor.matmul_mx(
-                    out=bank[:],
-                    lhsT=operand[0][:].bitcast(FP8X4),
-                    lhsT_scale=operand[1][:],
-                    rhs=words.bitcast(FP4X4),
-                    rhs_scale=voc_sc[:, j * BANK : (j + 1) * BANK],
-                    start=True,
-                    stop=True,
-                )
-                banks[j] = bank
-            return banks
+        def score(name, operand, j, bank_tag):
+            codes, scales = operand
+            bank = psum.tile([P, CHUNK], F32, name="%s_ps%d" % (name, j), tag=bank_tag)
+            words = voc_w[j // 2][:, (j % 2) * 2 * CHUNK : (j % 2 + 1) * 2 * CHUNK]
+            nc.tensor.matmul_mx(
+                out=bank[:],
+                lhsT=codes[:].bitcast(FP8X4),
+                lhsT_scale=scales[:],
+                rhs=words.bitcast(FP4X4),
+                rhs_scale=voc_sc[:, cols(j)],
+                start=True,
+                stop=True,
+            )
+            return bank
 
-        a_ps = scores("a", hq, ("bank0", "bank1", "bank2", "bank3"), range(NB))
-        ta_ps = scores("ta", dq, ("bank4", "bank5", "bank3", "bank4"), range(2))
+        a_ps = [score("a", hid_mx, j, "bank%d" % j) for j in range(CHUNKS)]
+        ta_ps = [score("ta", dhid_mx, j, TA_BANKS[j]) for j in range(TA_ON_SCALAR)]
 
-        def cols(j):
-            return slice(j * BANK, (j + 1) * BANK)
-
-        last = NB - 1
-        a_sb = keep.tile([P, V], F32, name="a_sb")
-        p_sb = keep.tile([P, V], F32, name="p_sb")
-        xp_sb = keep.tile([P, V], F32, name="xp_sb")
-        m_b = col("m_b", NB)
-        z_b = col("z_b", NB)
-        xz_b = col("xz_b", NB)
-        f_b = col("f_b", NB)
-        nc.vector.memset(f_b[:, last:NB], 1.0)
-        neg_m = col("neg_m")
-        for j in range(NB):
-            nc.vector.tensor_scalar(a_sb[:, cols(j)], a_ps[j][:], 1.0, None, ALU.mult, ALU.max, accum_out=m_b[:, j : j + 1])
-            if j < last:
-                shift = keep.tile([P, 1], F32, name="neg_m%d" % j, tag="shift%d" % j)
-                nc.gpsimd.tensor_scalar(shift[:], m_b[:, j : j + 1], -1.0, 0.0, ALU.mult, ALU.add)
+        a_sb = wide("a_sb", V)
+        p = wide("p", V)
+        xp = wide("xp", V)
+        chunk_max = wide("chunk_max", CHUNKS)
+        chunk_z = wide("chunk_z", CHUNKS)
+        chunk_xz = wide("chunk_xz", CHUNKS)
+        neg_m = wide("neg_m", 1)
+        for j in range(CHUNKS):
+            nc.vector.tensor_scalar(
+                a_sb[:, cols(j)], a_ps[j][:], 1.0, None, ALU.mult, ALU.max, accum_out=chunk_max[:, j : j + 1]
+            )
+            if j < LAST:
+                neg_max = wide("neg_max%d" % j, 1)
+                nc.gpsimd.tensor_scalar(neg_max[:], chunk_max[:, j : j + 1], -1.0, 0.0, ALU.mult, ALU.add)
             else:
-                shift = neg_m
-                nc.vector.tensor_reduce(neg_m[:], m_b[:], AX.X, ALU.max, negate=True)
-            nc.scalar.activation(p_sb[:, cols(j)], a_sb[:, cols(j)], ACT.Exp, bias=shift[:], accum_out=z_b[:, j : j + 1])
+                neg_max = neg_m
+                nc.vector.tensor_reduce(neg_m[:], chunk_max[:], AX.X, ALU.max, negate=True)
+            nc.scalar.activation(
+                p[:, cols(j)], a_sb[:, cols(j)], ACT.Exp, bias=neg_max[:], accum_out=chunk_z[:, j : j + 1]
+            )
 
-        neg_2th = keep.tile([P, 1], F32, name="neg_2th", tag="shift%d" % (last - 1))
-        nc.gpsimd.tensor_scalar(neg_2th[:], th_c[:], -2.0, 1.0, ALU.mult, ALU.mult)
-        a_x = keep.tile([P, I], F32, name="a_x")
-        nc.vector.tensor_copy(a_x[:], a_sb[:].indirect(offsets[:]))
-        nc.scalar.activation(f_b[:, :last], m_b[:, :last], ACT.Exp, bias=neg_m[:])
-        px = keep.tile([P, I], F32, name="px")
-        nc.scalar.activation(px[:], a_x[:], ACT.Exp, bias=neg_m[:])
-        preload = col("preload")
-        nc.scalar.activation(preload[:], px[:, 0:1], ACT.Abs_reciprocal_sqrt, bias=f_b[:, last:NB])
-        ta_sb = keep.tile([P, V], F32, name="ta_sb")
+        neg_2th = wide("neg_2th", 1, tag="neg_max%d" % (LAST - 1))
+        nc.gpsimd.tensor_scalar(neg_2th[:], th_col[:], -2.0, 1.0, ALU.mult, ALU.mult)
+        ax = wide("ax", I)
+        nc.vector.tensor_copy(ax[:], a_sb[:].indirect(offsets[:]))
+        nc.scalar.activation(f[:, :LAST], chunk_max[:, :LAST], ACT.Exp, bias=neg_m[:])
+        px = wide("px", I)
+        nc.scalar.activation(px[:], ax[:], ACT.Exp, bias=neg_m[:])
+        table_preload = wide("table_preload", 1)
+        nc.scalar.activation(table_preload[:], px[:, 0:1], ACT.Abs_reciprocal_sqrt, bias=f[:, LAST:CHUNKS])
+        ta_sb = wide("ta_sb", V)
         for j in range(TA_ON_SCALAR):
             nc.scalar.copy(ta_sb[:, cols(j)], ta_ps[j][:])
 
-        ta_tags = ("bank4", "bank5", "bank3", "bank4")
-        ta_ps[2] = scores("ta", dq, ta_tags, range(2, 3))[2]
-        nc.vector.tensor_copy(ta_sb[:, cols(2)], ta_ps[2][:])
+        def score_and_copy_ta(j):
+            ta_ps.append(score("ta", dhid_mx, j, TA_BANKS[j]))
+            nc.vector.tensor_copy(ta_sb[:, cols(j)], ta_ps[j][:])
 
-        fz_tmp = col("fz_tmp", NB)
-        neg_z = col("neg_z")
-        nc.vector.scalar_tensor_tensor(fz_tmp[:], f_b[:], -1.0, z_b[:], ALU.mult, ALU.mult, accum_out=neg_z[:])
-        c = col("c")
-        nc.gpsimd.tensor_scalar(c[:], neg_z[:], th_c[:], -1.0, ALU.mult, ALU.mult)
-        slope = col("slope")
+        score_and_copy_ta(TA_ON_SCALAR)
+
+        neg_fz = wide("neg_fz", CHUNKS)
+        neg_z = wide("neg_z", 1)
+        nc.vector.scalar_tensor_tensor(neg_fz[:], f[:], -1.0, chunk_z[:], ALU.mult, ALU.mult, accum_out=neg_z[:])
+        c = wide("c", 1)
+        nc.gpsimd.tensor_scalar(c[:], neg_z[:], th_col[:], -1.0, ALU.mult, ALU.mult)
+        slope = wide("slope", 1)
         nc.gpsimd.tensor_scalar(slope[:], neg_z[:], neg_z[:], neg_2th[:], ALU.mult, ALU.mult)
-        spx = keep.tile([P, I], F32, name="spx", tag="th_then_spx")
-        nc.gpsimd.tensor_tensor(spx[:], px[:], sw_b[:], ALU.mult)
-        shift_c = col("shift_c")
-        nc.gpsimd.tensor_scalar(shift_c[:], slope[:], c[:], 1.0, ALU.mult, ALU.mult)
+        sw_px = wide("sw_px", I, tag="th_then_sw_px")
+        nc.gpsimd.tensor_tensor(sw_px[:], px[:], sw_rows[:], ALU.mult)
+        slope_c = wide("slope_c", 1)
+        nc.gpsimd.tensor_scalar(slope_c[:], slope[:], c[:], 1.0, ALU.mult, ALU.mult)
 
-        r_root = keep.tile([P, I], F32, name="r_root", tag="root_then_cd")
-        r_abs = keep.tile([P, I], F32, name="r_abs")
-        r_sq = keep.tile([P, I], F32, name="r_sq")
-        halves = (slice(0, I // 2), slice(I // 2, I))
-        for half in halves:
-            nc.scalar.activation(r_root[:, half], px[:, half], ACT.Abs_reciprocal_sqrt, bias=c[:])
-        for half in halves:
-            nc.scalar.activation(r_abs[:, half], r_root[:, half], ACT.Square)
-        for half in halves:
-            nc.scalar.activation(r_sq[:, half], r_abs[:, half], ACT.Square)
-        cd = keep.tile([P, I], F32, name="cd", tag="root_then_cd")
-        nc.scalar.activation(cd[:], px[:], ACT.Identity, scale=slope[:], bias=shift_c[:])
+        inv_root = wide("inv_root", I, tag="inv_root_then_slope_d")
+        inv_abs = wide("inv_abs", I)
+        inv_sq = wide("inv_sq", I)
+        slot_halves = (slice(0, I // 2), slice(I // 2, I))
+        for slots in slot_halves:
+            nc.scalar.activation(inv_root[:, slots], px[:, slots], ACT.Abs_reciprocal_sqrt, bias=c[:])
+        for slots in slot_halves:
+            nc.scalar.activation(inv_abs[:, slots], inv_root[:, slots], ACT.Square)
+        for slots in slot_halves:
+            nc.scalar.activation(inv_sq[:, slots], inv_abs[:, slots], ACT.Square)
+        slope_d = wide("slope_d", I, tag="inv_root_then_slope_d")
+        nc.scalar.activation(slope_d[:], px[:], ACT.Identity, scale=slope[:], bias=slope_c[:])
 
-        banks = dict(ta_ps)
-        for j in range(NB):
-            if j == last:
-                banks[j] = scores("ta", dq, ta_tags, range(last, NB))[last]
-                nc.vector.tensor_copy(ta_sb[:, cols(j)], banks[j][:])
+        for j in range(CHUNKS):
+            if j == LAST:
+                score_and_copy_ta(LAST)
             nc.vector.scalar_tensor_tensor(
-                xp_sb[:, cols(j)], banks[j][:], f_b[:, j : j + 1], p_sb[:, cols(j)], ALU.mult, ALU.mult,
-                accum_out=xz_b[:, j : j + 1],
+                xp[:, cols(j)], ta_ps[j][:], f[:, j : j + 1], p[:, cols(j)], ALU.mult, ALU.mult,
+                accum_out=chunk_xz[:, j : j + 1],
             )
-        t_x = keep.tile([P, I], F32, name="t_x")
-        nc.vector.tensor_copy(t_x[:], ta_sb[:].indirect(offsets[:]))
-        neg_rz = col("neg_rz")
-        nc.vector.reciprocal(neg_rz[:], neg_z[:])
-        k_tmp = col("k_tmp", NB)
-        neg_k = col("neg_k")
-        nc.vector.tensor_scalar(k_tmp[:], xz_b[:], neg_rz[:], None, ALU.mult, ALU.add, accum_out=neg_k[:])
+        tx = wide("tx", I)
+        nc.vector.tensor_copy(tx[:], ta_sb[:].indirect(offsets[:]))
+        neg_inv_z = wide("neg_inv_z", 1)
+        nc.vector.reciprocal(neg_inv_z[:], neg_z[:])
+        chunk_neg_k = wide("chunk_neg_k", CHUNKS)
+        neg_k = wide("neg_k", 1)
+        nc.vector.tensor_scalar(chunk_neg_k[:], chunk_xz[:], neg_inv_z[:], None, ALU.mult, ALU.add, accum_out=neg_k[:])
 
-        g = keep.tile([P, I], F32, name="g")
-        b_row = col("b_row")
-        nc.vector.scalar_tensor_tensor(g[:], spx[:], neg_2th[:], r_sq[:], ALU.mult, ALU.mult, accum_out=b_row[:])
-        w = keep.tile([P, I], F32, name="w")
-        nc.vector.tensor_tensor(w[:], cd[:], r_sq[:], ALU.mult)
-        h = keep.tile([P, I], F32, name="h")
-        nc.vector.scalar_tensor_tensor(h[:], t_x[:], neg_k[:], g[:], ALU.add, ALU.mult)
-        xe2 = keep.tile([P, I], F32, name="xe2")
-        s2 = col("s2")
-        nc.vector.scalar_tensor_tensor(xe2[:], w[:], neg_z[:], h[:], ALU.subtract, ALU.mult, accum_out=s2[:])
-        nc.vector.tensor_copy(xs[:].indirect(offsets[:]), xe2[:])
+        g = wide("g", I)
+        b = wide("b", 1)
+        nc.vector.scalar_tensor_tensor(g[:], sw_px[:], neg_2th[:], inv_sq[:], ALU.mult, ALU.mult, accum_out=b[:])
+        w = wide("w", I)
+        nc.vector.tensor_tensor(w[:], slope_d[:], inv_sq[:], ALU.mult)
+        centred_g = wide("centred_g", I)
+        nc.vector.scalar_tensor_tensor(centred_g[:], tx[:], neg_k[:], g[:], ALU.add, ALU.mult)
+        xe2 = wide("xe2", I)
+        s = wide("s", 1)
+        nc.vector.scalar_tensor_tensor(xe2[:], w[:], neg_z[:], centred_g[:], ALU.subtract, ALU.mult, accum_out=s[:])
+        nc.vector.tensor_copy(scattered[:].indirect(offsets[:]), xe2[:])
 
-        def base_cols(j):
-            return base_sb[j // 2][:, (j % 2) * BANK : (j % 2 + 1) * BANK]
+        b_xp = wide("b_xp", V)
+        for span in (slice(CHUNK, CHUNK + P), slice(CHUNK + P, 2 * CHUNK), cols(2), cols(3)):
+            nc.scalar.activation(b_xp[:, span], xp[:, span], ACT.Identity, scale=b[:])
+        neg_kb = wide("neg_kb", 1)
+        nc.scalar.activation(neg_kb[:], neg_k[:], ACT.Identity, scale=b[:])
+        p_factor = wide("p_factor", 1, tag="turned2")
+        nc.scalar.activation(p_factor[:], neg_inv_z[:], ACT.Identity, scale=s[:], bias=neg_kb[:])
+        p_term_last = wide("p_term_last", CHUNK)
+        nc.scalar.activation(p_term_last[:], p[:, cols(LAST)], ACT.Identity, scale=p_factor[:])
+        chunk_p_factor = wide("chunk_p_factor", CHUNKS)
+        nc.scalar.activation(chunk_p_factor[:], f[:], ACT.Identity, scale=p_factor[:])
 
-        def block(ap, b):
-            return ap[:, b * P : (b + 1) * P]
-
-        bxp = keep.tile([P, V], F32, name="bxp")
-        for j in TWO_TERMS + THREE_TERMS:
-            nc.scalar.activation(bxp[:, cols(j)], xp_sb[:, cols(j)], ACT.Identity, scale=b_row[:])
-        kb = col("kb")
-        nc.scalar.activation(kb[:], neg_k[:], ACT.Identity, scale=b_row[:])
-        a_row = col("a_row")
-        nc.scalar.activation(a_row[:], neg_rz[:], ACT.Identity, scale=s2[:], bias=kb[:])
-        ap = keep.tile([P, V], F32, name="ap")
-        nc.scalar.activation(ap[:, cols(last)], p_sb[:, cols(last)], ACT.Identity, scale=a_row[:])
-        a_b = col("a_b", NB)
-        nc.scalar.activation(a_b[:], f_b[:], ACT.Identity, scale=a_row[:])
-
-        partial = {}
-        for j in ON_VECTOR:
-            partial[j] = keep.tile([P, BANK], F32, name="partial%d" % j)
-            nc.vector.scalar_tensor_tensor(partial[j][:], xp_sb[:, cols(j)], b_row[:], base_cols(j), ALU.mult, ALU.add)
-
-        for j in TWO_TERMS + THREE_TERMS:
-            terms = [base_cols(j), bxp[:, cols(j)]] + ([ap[:, cols(j)]] if j in THREE_TERMS else [])
-            turned = psum.tile([P, BANK], F32, name="turned%d" % j, tag="bank%d" % (j - 1))
-            for b in range(BANK // P):
-                for n, term in enumerate(terms):
+        partial = [wide("partial0", CHUNK)]
+        nc.vector.scalar_tensor_tensor(partial[0][:], xp[:, cols(0)], b[:], base_chunk(0), ALU.mult, ALU.add)
+        for j in range(1, CHUNKS):
+            terms = [base_chunk(j), b_xp[:, cols(j)]] + ([p_term_last[:]] if j == LAST else [])
+            turned_ps = psum.tile([P, CHUNK], F32, name="turned_ps%d" % j, tag="bank%d" % (j - 1))
+            for n in range(CHUNK // P):
+                for t, term in enumerate(terms):
                     nc.tensor.matmul(
-                        block(turned, b), block(term, b), ident[:],
-                        start=(n == 0), stop=(n == len(terms) - 1), is_transpose=True,
+                        block(turned_ps, n), block(term, n), ident[:],
+                        start=(t == 0), stop=(t == len(terms) - 1), is_transpose=True,
                     )
-            turned_sb = keep.tile([P, BANK], F32, name="turned_sb%d" % j, tag="turned_then_res%d" % j)
-            nc.scalar.copy(turned_sb[:], turned[:])
-            partial[j] = psum.tile([P, BANK], F32, name="partial_ps%d" % j, tag="bank%d" % (j + 4))
-            for b in range(BANK // P):
-                nc.tensor.transpose(block(partial[j], b), block(turned_sb, b), ident[:])
+            turned = wide("turned%d" % j, CHUNK)
+            for lo in (0, HALF):
+                nc.scalar.copy(turned[:, lo : lo + HALF], turned_ps[:, lo : lo + HALF])
+            partial.append(psum.tile([P, CHUNK], F32, name="partial_ps%d" % j, tag="bank%d" % (j + 4)))
+            for n in range(CHUNK // P):
+                nc.tensor.transpose(block(partial[j], n), block(turned, n), ident[:])
 
-        dense = keep.tile([P, V], F32, name="dense")
+        result = wide("result", V)
+        result0 = wide("result0", CHUNK, tag="turned1")
+        dense = [wide("dense0", CHUNK), wide("dense1", CHUNK), wide("dense2", CHUNK, tag="turned3")]
 
-        def add_p(j):
+        def add_p_term(j, lo, hi):
             nc.vector.scalar_tensor_tensor(
-                dense[:, cols(j)], p_sb[:, cols(j)], a_b[:, j : j + 1], partial[j][:], ALU.mult, ALU.add
+                dense[j][:, lo:hi], p[:, j * CHUNK + lo : j * CHUNK + hi], chunk_p_factor[:, j : j + 1],
+                partial[j][:, lo:hi], ALU.mult, ALU.add,
             )
 
-        def finish(j, src, tag, pieces):
-            res = keep.tile([P, BANK], F32, name="res%d" % j, tag=tag)
-            width = BANK // pieces
-            for lo in range(0, BANK, width):
-                span = slice(j * BANK + lo, j * BANK + lo + width)
-                nc.vector.tensor_tensor(res[:, lo : lo + width], src[:, lo : lo + width], xs[:, span], ALU.add)
-                nc.sync.dma_start(out=out[:, span], in_=res[:, lo : lo + width])
+        def add_scattered_and_store(j, dst, src, lo, hi):
+            span = slice(j * CHUNK + lo, j * CHUNK + hi)
+            nc.vector.tensor_tensor(dst[:, lo:hi], src[:, lo:hi], scattered[:, span], ALU.add)
+            nc.sync.dma_start(out=out[:, span], in_=dst[:, lo:hi])
 
-        add_p(0)
-        add_p(1)
-        finish(0, dense[:, cols(0)], "turned_then_res1", 1)
-        add_p(2)
-        finish(1, dense[:, cols(1)], "turned_then_res2", 1)
-        finish(3, partial[3], "res3", 1)
-        finish(2, dense[:, cols(2)], "turned_then_res3", 2)
+        add_p_term(0, 0, CHUNK)
+        add_p_term(1, 0, CHUNK)
+        add_scattered_and_store(0, result0, dense[0], 0, CHUNK)
+        add_scattered_and_store(1, result[:, cols(1)], dense[1], 0, CHUNK)
+        add_scattered_and_store(LAST, result[:, cols(LAST)], partial[LAST], 0, CHUNK)
+        for lo in (0, HALF):
+            add_p_term(2, lo, lo + HALF)
+        for lo in (0, HALF):
+            add_scattered_and_store(2, result[:, cols(2)], dense[2], lo, lo + HALF)

from contextlib import ExitStack

import concourse.mybir as mybir
from concourse.masks import make_identity

D, V, Q, I = 512, 2048, 128, 512
FLOPS = 2 * 2 * D * Q * V

F32 = mybir.dt.float32
BF16 = mybir.dt.bfloat16
I32 = mybir.dt.int32
U32 = mybir.dt.uint32
U16 = mybir.dt.uint16
U8 = mybir.dt.uint8
FP8X4 = mybir.dt.float8_e4m3fn_x4
FP4X4 = mybir.dt.float4_e2m1fn_x4
ALU = mybir.AluOpType
ACT = mybir.ActivationFunctionType
AX = mybir.AxisListType

P = 128
PACK = 4
CHUNK = 512
CHUNKS = V // CHUNK
LAST = CHUNKS - 1
HALF = CHUNK // 2
TA_BANKS = ("bank4", "bank5", "bank3", "bank4")
TA_ON_SCALAR = 2


def tile_attend_hvpresence_heads_kernel(tc, hid, voc_words, voc_scales, th, sw, dhid, base, offs, out):
    nc = tc.nc
    with ExitStack() as ctx:
        keep = ctx.enter_context(tc.tile_pool(name="keep", bufs=1))
        psum = ctx.enter_context(tc.psum_pool(name="psum", bufs=1))

        def wide(name, width, tag=""):
            return keep.tile([P, width], F32, name=name, tag=tag or name)

        def cols(j):
            return slice(j * CHUNK, (j + 1) * CHUNK)

        def block(rows, n):
            return rows[:, n * P : (n + 1) * P]

        voc_sc = keep.tile([P, V], U8, name="voc_sc", align_bytes=64)
        nc.gpsimd.memset(voc_sc[:].bitcast(I32), 0)
        zero = wide("zero", 1)
        f = wide("f", CHUNKS)
        nc.vector.memset(zero[:], 0.0)
        nc.scalar.activation(f[:, LAST:CHUNKS], zero[:], ACT.Exp)
        scattered = wide("scattered", V)
        nc.vector.memset(scattered[:], 0.0)
        ident = wide("ident", P)
        make_identity(nc, ident[:])

        hid_raw = keep.tile([P, PACK, Q], F32, name="hid_raw")
        nc.sync.dma_start(out=hid_raw[:], in_=hid.rearrange("(p t) q -> p t q", t=PACK))
        voc_w = [keep.tile([P, V], U8, name="voc_w%d" % half, align_bytes=64) for half in range(2)]

        def load_words(half):
            nc.sync.dma_start(out=voc_w[half][:].bitcast(I32), in_=voc_words[0, :, half * V : (half + 1) * V].bitcast(I32))

        load_words(0)
        for quadrant in range(4):
            nc.sync.dma_start(
                out=voc_sc[32 * quadrant : 32 * quadrant + 4, :].bitcast(I32),
                in_=voc_scales[0, 4 * quadrant : 4 * quadrant + 4, :].bitcast(I32),
            )
        dhid_raw = keep.tile([P, PACK, Q], F32, name="dhid_raw")
        nc.sync.dma_start(out=dhid_raw[:], in_=dhid.rearrange("(p t) q -> p t q", t=PACK))
        load_words(1)
        offsets = keep.tile([P, I // 16], U16, name="offsets")
        nc.sync.dma_start(offsets[:], offs)
        th_col = wide("th_col", 1, tag="th_then_sw_px")
        nc.sync.dma_start(out=th_col[:], in_=th)
        sw_rows = wide("sw_rows", I)
        nc.sync.dma_start(out=sw_rows[:], in_=sw[0].partition_broadcast(P))
        base_halves = []
        for half in range(2):
            base_half = wide("base%d" % half, V // 2)
            nc.sync.dma_start(out=base_half[:], in_=base[:, half * (V // 2) : (half + 1) * (V // 2)])
            base_halves.append(base_half)

        def base_chunk(j):
            return base_halves[j // 2][:, cols(j % 2)]

        def quantise(name, raw, copy):
            grouped = keep.tile([P, Q, PACK], BF16, name=name + "_grouped", align_bytes=64)
            copy(grouped[:], raw[:].rearrange("p t q -> p q t"))
            codes = keep.tile([P, Q], U32, name=name + "_codes", align_bytes=64)
            scales = keep.tile([P, Q], U8, name=name + "_scales", align_bytes=64)
            nc.vector.quantize_mx(out=codes[:].bitcast(FP8X4), scales=scales[:], in_=grouped[:].rearrange("p q t -> p (q t)"))
            return codes, scales

        hid_mx = quantise("hid", hid_raw, nc.vector.tensor_copy)
        dhid_mx = quantise("dhid", dhid_raw, nc.scalar.copy)

        def score(name, operand, j, bank_tag):
            codes, scales = operand
            bank = psum.tile([P, CHUNK], F32, name="%s_ps%d" % (name, j), tag=bank_tag)
            words = voc_w[j // 2][:, (j % 2) * 2 * CHUNK : (j % 2 + 1) * 2 * CHUNK]
            nc.tensor.matmul_mx(
                out=bank[:],
                lhsT=codes[:].bitcast(FP8X4),
                lhsT_scale=scales[:],
                rhs=words.bitcast(FP4X4),
                rhs_scale=voc_sc[:, cols(j)],
                start=True,
                stop=True,
            )
            return bank

        a_ps = [score("a", hid_mx, j, "bank%d" % j) for j in range(CHUNKS)]
        ta_ps = [score("ta", dhid_mx, j, TA_BANKS[j]) for j in range(TA_ON_SCALAR)]

        a_sb = wide("a_sb", V)
        p = wide("p", V)
        xp = wide("xp", V)
        chunk_max = wide("chunk_max", CHUNKS)
        chunk_z = wide("chunk_z", CHUNKS)
        chunk_xz = wide("chunk_xz", CHUNKS)
        neg_m = wide("neg_m", 1)
        for j in range(CHUNKS):
            nc.vector.tensor_scalar(
                a_sb[:, cols(j)], a_ps[j][:], 1.0, None, ALU.mult, ALU.max, accum_out=chunk_max[:, j : j + 1]
            )
            if j < LAST:
                neg_max = wide("neg_max%d" % j, 1)
                nc.gpsimd.tensor_scalar(neg_max[:], chunk_max[:, j : j + 1], -1.0, 0.0, ALU.mult, ALU.add)
            else:
                neg_max = neg_m
                nc.vector.tensor_reduce(neg_m[:], chunk_max[:], AX.X, ALU.max, negate=True)
            nc.scalar.activation(
                p[:, cols(j)], a_sb[:, cols(j)], ACT.Exp, bias=neg_max[:], accum_out=chunk_z[:, j : j + 1]
            )

        neg_2th = wide("neg_2th", 1, tag="neg_max%d" % (LAST - 1))
        nc.gpsimd.tensor_scalar(neg_2th[:], th_col[:], -2.0, 1.0, ALU.mult, ALU.mult)
        ax = wide("ax", I)
        nc.vector.tensor_copy(ax[:], a_sb[:].indirect(offsets[:]))
        nc.scalar.activation(f[:, :LAST], chunk_max[:, :LAST], ACT.Exp, bias=neg_m[:])
        px = wide("px", I)
        nc.scalar.activation(px[:], ax[:], ACT.Exp, bias=neg_m[:])
        table_preload = wide("table_preload", 1)
        nc.scalar.activation(table_preload[:], px[:, 0:1], ACT.Abs_reciprocal_sqrt, bias=f[:, LAST:CHUNKS])
        ta_sb = wide("ta_sb", V)
        for j in range(TA_ON_SCALAR):
            nc.scalar.copy(ta_sb[:, cols(j)], ta_ps[j][:])

        def score_and_copy_ta(j):
            ta_ps.append(score("ta", dhid_mx, j, TA_BANKS[j]))
            nc.vector.tensor_copy(ta_sb[:, cols(j)], ta_ps[j][:])

        score_and_copy_ta(TA_ON_SCALAR)

        neg_fz = wide("neg_fz", CHUNKS)
        neg_z = wide("neg_z", 1)
        nc.vector.scalar_tensor_tensor(neg_fz[:], f[:], -1.0, chunk_z[:], ALU.mult, ALU.mult, accum_out=neg_z[:])
        c = wide("c", 1)
        nc.gpsimd.tensor_scalar(c[:], neg_z[:], th_col[:], -1.0, ALU.mult, ALU.mult)
        slope = wide("slope", 1)
        nc.gpsimd.tensor_scalar(slope[:], neg_z[:], neg_z[:], neg_2th[:], ALU.mult, ALU.mult)
        sw_px = wide("sw_px", I, tag="th_then_sw_px")
        nc.gpsimd.tensor_tensor(sw_px[:], px[:], sw_rows[:], ALU.mult)
        slope_c = wide("slope_c", 1)
        nc.gpsimd.tensor_scalar(slope_c[:], slope[:], c[:], 1.0, ALU.mult, ALU.mult)

        inv_root = wide("inv_root", I, tag="inv_root_then_slope_d")
        inv_abs = wide("inv_abs", I)
        inv_sq = wide("inv_sq", I)
        slot_halves = (slice(0, I // 2), slice(I // 2, I))
        for slots in slot_halves:
            nc.scalar.activation(inv_root[:, slots], px[:, slots], ACT.Abs_reciprocal_sqrt, bias=c[:])
        for slots in slot_halves:
            nc.scalar.activation(inv_abs[:, slots], inv_root[:, slots], ACT.Square)
        for slots in slot_halves:
            nc.scalar.activation(inv_sq[:, slots], inv_abs[:, slots], ACT.Square)
        slope_d = wide("slope_d", I, tag="inv_root_then_slope_d")
        nc.scalar.activation(slope_d[:], px[:], ACT.Identity, scale=slope[:], bias=slope_c[:])

        for j in range(CHUNKS):
            if j == LAST:
                score_and_copy_ta(LAST)
            nc.vector.scalar_tensor_tensor(
                xp[:, cols(j)], ta_ps[j][:], f[:, j : j + 1], p[:, cols(j)], ALU.mult, ALU.mult,
                accum_out=chunk_xz[:, j : j + 1],
            )
        tx = wide("tx", I)
        nc.vector.tensor_copy(tx[:], ta_sb[:].indirect(offsets[:]))
        neg_inv_z = wide("neg_inv_z", 1)
        nc.vector.reciprocal(neg_inv_z[:], neg_z[:])
        chunk_neg_k = wide("chunk_neg_k", CHUNKS)
        neg_k = wide("neg_k", 1)
        nc.vector.tensor_scalar(chunk_neg_k[:], chunk_xz[:], neg_inv_z[:], None, ALU.mult, ALU.add, accum_out=neg_k[:])

        g = wide("g", I)
        b = wide("b", 1)
        nc.vector.scalar_tensor_tensor(g[:], sw_px[:], neg_2th[:], inv_sq[:], ALU.mult, ALU.mult, accum_out=b[:])
        w = wide("w", I)
        nc.vector.tensor_tensor(w[:], slope_d[:], inv_sq[:], ALU.mult)
        centred_g = wide("centred_g", I)
        nc.vector.scalar_tensor_tensor(centred_g[:], tx[:], neg_k[:], g[:], ALU.add, ALU.mult)
        xe2 = wide("xe2", I)
        s = wide("s", 1)
        nc.vector.scalar_tensor_tensor(xe2[:], w[:], neg_z[:], centred_g[:], ALU.subtract, ALU.mult, accum_out=s[:])
        nc.vector.tensor_copy(scattered[:].indirect(offsets[:]), xe2[:])

        b_xp = wide("b_xp", V)
        for span in (slice(CHUNK, CHUNK + P), slice(CHUNK + P, 2 * CHUNK), cols(2), cols(3)):
            nc.scalar.activation(b_xp[:, span], xp[:, span], ACT.Identity, scale=b[:])
        neg_kb = wide("neg_kb", 1)
        nc.scalar.activation(neg_kb[:], neg_k[:], ACT.Identity, scale=b[:])
        p_factor = wide("p_factor", 1, tag="turned2")
        nc.scalar.activation(p_factor[:], neg_inv_z[:], ACT.Identity, scale=s[:], bias=neg_kb[:])
        p_term_last = wide("p_term_last", CHUNK)
        nc.scalar.activation(p_term_last[:], p[:, cols(LAST)], ACT.Identity, scale=p_factor[:])
        chunk_p_factor = wide("chunk_p_factor", CHUNKS)
        nc.scalar.activation(chunk_p_factor[:], f[:], ACT.Identity, scale=p_factor[:])

        partial = [wide("partial0", CHUNK)]
        nc.vector.scalar_tensor_tensor(partial[0][:], xp[:, cols(0)], b[:], base_chunk(0), ALU.mult, ALU.add)
        for j in range(1, CHUNKS):
            terms = [base_chunk(j), b_xp[:, cols(j)]] + ([p_term_last[:]] if j == LAST else [])
            turned_ps = psum.tile([P, CHUNK], F32, name="turned_ps%d" % j, tag="bank%d" % (j - 1))
            for n in range(CHUNK // P):
                for t, term in enumerate(terms):
                    nc.tensor.matmul(
                        block(turned_ps, n), block(term, n), ident[:],
                        start=(t == 0), stop=(t == len(terms) - 1), is_transpose=True,
                    )
            turned = wide("turned%d" % j, CHUNK)
            for lo in (0, HALF):
                nc.scalar.copy(turned[:, lo : lo + HALF], turned_ps[:, lo : lo + HALF])
            partial.append(psum.tile([P, CHUNK], F32, name="partial_ps%d" % j, tag="bank%d" % (j + 4)))
            for n in range(CHUNK // P):
                nc.tensor.transpose(block(partial[j], n), block(turned, n), ident[:])

        result = wide("result", V)
        result0 = wide("result0", CHUNK, tag="turned1")
        dense = [wide("dense0", CHUNK), wide("dense1", CHUNK), wide("dense2", CHUNK, tag="turned3")]

        def add_p_term(j, lo, hi):
            nc.vector.scalar_tensor_tensor(
                dense[j][:, lo:hi], p[:, j * CHUNK + lo : j * CHUNK + hi], chunk_p_factor[:, j : j + 1],
                partial[j][:, lo:hi], ALU.mult, ALU.add,
            )

        def add_scattered_and_store(j, dst, src, lo, hi):
            span = slice(j * CHUNK + lo, j * CHUNK + hi)
            nc.vector.tensor_tensor(dst[:, lo:hi], src[:, lo:hi], scattered[:, span], ALU.add)
            nc.sync.dma_start(out=out[:, span], in_=dst[:, lo:hi])

        add_p_term(0, 0, CHUNK)
        add_p_term(1, 0, CHUNK)
        add_scattered_and_store(0, result0, dense[0], 0, CHUNK)
        add_scattered_and_store(1, result[:, cols(1)], dense[1], 0, CHUNK)
        add_scattered_and_store(LAST, result[:, cols(LAST)], partial[LAST], 0, CHUNK)
        for lo in (0, HALF):
            add_p_term(2, lo, lo + HALF)
        for lo in (0, HALF):
            add_scattered_and_store(2, result[:, cols(2)], dense[2], lo, lo + HALF)
